import numpy as np, ml_dtypes
CORES = [8,136,40,168]
N = 4
BF = ml_dtypes.bfloat16
def gentries(a):
    return np.ascontiguousarray(a.reshape(8, 16, -1).transpose(0, 2, 1)).reshape(8, -1)
def gtable(e):
    e = np.asarray(e); return np.ascontiguousarray(e.reshape(8, -1, 16).transpose(0, 2, 1)).reshape(128, -1).astype(np.int32)
W, SB, P, HOPS, STEP, GAIN = 2048, 11, 192, 5, 3, 8
def parts(rng):
    x = rng.integers(0, 64, (N, 8, 16, W)); n = rng.integers(0, W, (N, 8, 16, W))
    s = rng.integers(0, rng.integers(2, 9, (N, 8, 1, W)) + 1, (N, 8, 16, W))
    return x, n, s, rng.integers(0, W, (N, 8, P)), rng.integers(0, 64, (N, 8, 16, P)), rng.integers(1, 256, (N, 8, 16, 1))
def lonely(rng, n, s, v, old, few, start):
    for q in range(N):
        for g in range(8):
            o = rng.permutation(W); a = o[:old]; b = o[old:old + few]
            s[q, g][:, a] = 0; n[q, g][:, b] = a[rng.integers(0, old, (16, few))]
            v[q, g, rng.permutation(P)[:start]] = b[rng.integers(0, few, start)]
def scarce(rng, n, s, v):
    lone = np.zeros((N, 8), np.int64); sh = int(rng.integers(0, 4))
    for q in range(N):
        for g in range(8):
            a, b = [int(m) for m in rng.permutation(W)[:2]]
            n[q, g][:, a] = b; s[q, g][:, b] = 0; lone[q, g] = a
    live = np.any(np.take_along_axis(s, n, 3) > 0, axis=2)
    for q in range(N):
        for g in range(8):
            c = np.flatnonzero(live[q, g])
            v[q, g] = np.where(live[q, g, v[q, g]], v[q, g], c[rng.integers(0, len(c), P)])
        for m in rng.permutation(8 * P)[:(q + sh) & 3]:
            g = int(m) // P; v[q, g, int(m) - g * P] = lone[q, g]
def plant(rng, x, n, s, v, z):
    for q in range(N):
        for g in range(8):
            o = [int(m) for m in 1 + rng.permutation(W - 1)[:25]]; X, M, S, Z = x[q, g], n[q, g], s[q, g], z[q, g]
            a, b, c = o[:3]
            M[:, 0] = c; S[:, c] = 0; Z[:, 0] = 0; v[q, g, 0] = 0
            M[:, a] = b; M[:, b] = 0; S[:, b] = rng.integers(1, 9, 16); v[q, g, 1] = a
            for p, j in ((2, 3), (P - 1, 9)):
                a, b, c, d1, d2, d3 = o[j:j + 6]; r = 63 * rng.integers(0, 2, 16)
                Z[:, p] = r; v[q, g, p] = a; M[:, a] = c; M[0, a] = b
                S[:, b] = rng.integers(1, 9, 16); S[15, b] = 0; M[0, b] = d3
                S[:, c] = rng.integers(1, 9, 16); M[:, c] = d1; M[15, c] = d2
                X[:, d1] = r; X[:, d2] = r; X[:, d3] = r; X[15, d1] = r[15] ^ 1
            for p, j in ((3, 15), (P - 2, 20)):
                a, b, c, d, h = o[j:j + 5]; r = 63 * rng.integers(0, 2, 16); k = int(rng.integers(1, 16))
                Z[:, p] = r; v[q, g, p] = a; M[:, a] = c; M[0, a] = b
                S[:, b] = rng.integers(1, 9, 16); S[0, b] = 0; M[0, b] = d; X[:, d] = r
                S[:, c] = 0; S[k, c] = int(rng.integers(1, 9)); M[k, c] = h; X[:, h] = 63 - r
def pack(x, e, v, z, w):
    return {"xs": np.ascontiguousarray(x.reshape(N, 128, W)).astype(np.float32).astype(BF), "en": np.ascontiguousarray(e.reshape(N, 128, W)).astype(np.int32),
            "v0": np.stack([gtable(a) for a in v]), "z0": np.ascontiguousarray(z.reshape(N, 128, P)).astype(np.float32).astype(BF), "wt": np.ascontiguousarray(w.reshape(N, 128, 1)).astype(np.int32)}
def setup_inputs(rng):
    x, n, s, v, z, w = parts(rng)
    lonely(rng, n, s, v, W // 8, W // 16, P // 8)
    return pack(x, n + W * s, v, z, w)
def setup_inputs_spread(rng):
    x, n, s, v, z, w = parts(rng)
    ex = rng.choice(np.array([0.25, 1.0, 4.0]), (N, 8, 1, W)); es = rng.choice(np.array([0.25, 1.0, 4.0]), (N, 8, 1, W)); en = rng.choice(np.array([1.0, 3.0]), (N, 8, 1, W))
    x = (64 * rng.random(x.shape) ** ex).astype(np.int64); s = (9 * rng.random(x.shape) ** es).astype(np.int64); n = (W * rng.random(x.shape) ** en).astype(np.int64)
    x = np.minimum(x, 63); s = np.minimum(s, 8); n = np.minimum(n, W - 1)
    v = np.minimum((W * rng.random(v.shape) ** 2).astype(np.int64), W - 1)
    z = np.minimum((64 * rng.random(z.shape) ** rng.choice(np.array([0.25, 1.0, 4.0]), (N, 8, 1, P))).astype(np.int64), 63)
    w = np.minimum(1 + (255 * rng.random(w.shape) ** 4).astype(np.int64), 255)
    scarce(rng, n, s, v)
    return pack(x, n + W * s, v, z, w)
def setup_inputs_ends(rng):
    x, n, s, v, z, w = parts(rng); hi = 9 * W - 1
    x = 63 * rng.integers(0, 2, x.shape); z = 63 * rng.integers(0, 2, z.shape); w = 1 + 254 * rng.integers(0, 2, w.shape); v = (W - 1) * rng.integers(0, 2, v.shape)
    e = np.where(rng.random(x.shape) < 0.8, hi * rng.integers(0, 2, x.shape), rng.choice(np.array([1, W - 2, 8 * W, 8 * W + 1, 9 * W - 2]), x.shape))
    e[..., W - 1] = rng.choice(np.array([hi, hi, 8 * W + 1, 9 * W - 2]), (N, 8, 16)); e[:, :, 15, W - 1] = hi
    e[..., W - 3] = 0; e[:, 7, :, W - 4] = hi
    one = rng.integers(0, 16, (N, 8)); one[:, 7] = 15; one[N - 1] = 15
    e[..., 0] = np.where(np.arange(16) == one[..., None], hi, 0)
    full = 63 * rng.integers(0, 2, (N, 8, 1)); full[:, 7] = 63
    for c in (1, W - 2, W - 1): x[..., c] = full
    for p in (0, P - 1): z[..., p] = full
    for p in (1, P - 2, P - 3): z[..., p] = 63 - full
    for p in (0, 1, P - 2, P - 1): v[..., p] = W - 1
    v[..., 2] = 0; v[..., P - 3] = W - 3; w[:, 7] = 255; w[:, 0, 0] = 1
    return pack(x, e, v, z, w)
def setup_inputs_corners(rng):
    x, n, s, v, z, w = parts(rng); o = [int(a) for a in rng.permutation(8)]; col = np.arange(W); i = np.arange(16)[:, None]
    n[:, o[0]] = col
    k = rng.integers(0, 4, (N, 16, W))
    n[:, o[1]] = np.where(k == 0, 0, np.where(k == 1, W - 1, np.where(k == 2, col, (col + 1) & (W - 1))))
    h = P // 2; s[:, o[2]] = 0; w[:, o[2], 0] = 255; w[:, o[2], 1] = W // 256 - 1
    z[:, o[2], :, :h] = 0; z[:, o[2], 0, :h] = W // 256; z[:, o[2], 1, :h] = 1
    s[:, o[3]] = np.where(i < 8, i + 1, 0)
    s[:, o[4]] = np.where(i == 0, 4, np.where(i == 12, 6, np.where(i == 13, 8, 0)))
    s[:, o[5]] = np.where(i == 0, 4, np.where(i == 13, 8, 0))
    for c in (3, 4, 5): x[:, o[c]] = np.repeat(x[:, o[c], :, :1], W, axis=2)
    s[::2, o[6]] = 8; s[1::2, o[6]] = 0
    v[..., 0] = W - 1; v[..., 1] = 0; v[..., P - 1] = W - 1
    for q in range(N):
        m = rng.permutation(W - 1); a = np.append(m[:P - 1], W - 1); b = m[P - 1:2 * P - 1]
        n[q, o[7]][:, a] = b; n[q, o[7]][:, b] = b; s[q, o[7]][:, b] = rng.integers(1, 9, (16, P)); v[q, o[7]] = a
    return pack(x, n + W * s, v, z, w)
def setup_inputs_crowd(rng):
    x, n, s, v, z, w = parts(rng)
    lonely(rng, n, s, v, W // 4, W // 4, 1)
    want = (8 * P, 8 * P - 1, 255, 256); sh = int(rng.integers(0, 4))
    for q in range(N):
        bad = np.zeros(8 * P, bool); bad[rng.permutation(8 * P)[:want[(q + sh) % 4]]] = True; bad = bad.reshape(8, P)
        for g in range(8):
            a, b, c, d, hub = [int(m) for m in rng.permutation(W)[:5]]
            n[q, g, :, a] = b; s[q, g, :, b] = 8
            if g % 3 == 0: n[q, g, :, b] = a
            if g % 3 == 1: n[q, g, :, b] = hub
            n[q, g, :, c] = d; s[q, g, :, d] = 0
            v[q, g] = np.where(bad[g], c, a)
    z[:, ::2] = np.repeat(z[:, ::2, :, :1], P, axis=3)
    return pack(x, n + W * s, v, z, w)
def setup_inputs_ties(rng):
    x, n, s, v, z, w = parts(rng)
    base = rng.integers(0, 16, (N, 8, 16, 1)); proto = rng.integers(0, 4, (N, 8, W))
    x = np.repeat(base, W, axis=3); x[:, :, 0] = base[:, :, 0] + GAIN * proto
    i = np.arange(16)[:, None]; s = (i + rng.integers(0, 8, (N, 8, 1, W))) & 7
    s = np.where((rng.random((N, 8, 1, W)) < 0.5) & (s == 0) & (i < 8), 8, s)
    n = np.where(rng.random((N, 8, 1, W)) < 0.3, rng.integers(0, W, (N, 8, 1, W)), n)
    z[:, :, 0] = 63 * (rng.random((N, 8, P)) < 0.25)
    plant(rng, x, n, s, v, z)
    return pack(x, n + W * s, v, z, w)
def check_inputs(d):
    bad = []
    for k, lo, hi in (("xs", 0, 63), ("en", 0, 9 * W - 1), ("v0", 0, W - 1), ("z0", 0, 63), ("wt", 1, 255)):
        a = np.asarray(d[k]).astype(np.float64)
        if not (np.min(a) >= lo and np.max(a) <= hi): bad.append("range of " + k)
        elif np.any(a != np.floor(a)): bad.append("whole numbers of " + k)
    return bad
def reference(xs, en, v0, z0, wt):
    x = xs.astype(np.float32).astype(np.int64).reshape(N, 8, 16, W); e = en.astype(np.int64).reshape(N, 8, 16, W); w = wt.astype(np.int64).reshape(N, 8, 16, 1)
    v = np.stack([gentries(a) for a in v0]).astype(np.int64); z = z0.astype(np.float32).astype(np.int64).reshape(N, 8, 16, P)
    tau = np.zeros((N, 8, P), np.int64); A = np.zeros(N, np.int64); k16 = np.arange(16); pn = np.arange(P)
    qi = np.arange(N)[:, None, None]; gi = np.arange(8)[None, :, None]
    for t in range(HOPS):
        if t > 0: v = np.roll(v, STEP, axis=0); tau = np.roll(tau, STEP, axis=0); z = np.roll(z, STEP, axis=0)
        ring = np.take_along_axis(e, v[:, :, None, :], 3) & (W - 1)
        F = np.take_along_axis(e, ring.reshape(N, 8, 1, 16 * P), 3).reshape(N, 8, 16, 16, P)
        newer = np.count_nonzero((F >> SB) > tau[:, :, None, None, :], axis=2)
        fk = F[:, :, (k16 + t) & 15, k16]
        rec = np.take_along_axis(x, (fk & (W - 1)).reshape(N, 8, 1, 16 * P), 3).reshape(N, 8, 16, 16, P)
        score = np.add.reduce(np.abs(rec - z[:, :, :, None, :]), axis=2) - GAIN * newer
        ok = (k16[:, None] < 16 - tau[:, :, None, :]) & ((fk >> SB) > tau[:, :, None, :])
        best = np.argmin(np.where(ok, score, 2 ** 20), axis=2); found = np.any(ok, axis=2)
        fa = np.take_along_axis(fk, best[:, :, None, :], 2)[:, :, 0]
        u = np.add.reduce(w * z, axis=2) & (W - 1)
        f = np.where(found, fa & (W - 1), ((u * u >> 5) + 37 * u + A[:, None, None]) & (W - 1))
        tau = np.where(found, fa >> SB, 0)
        z = np.where(found[:, :, None, :], z, np.abs(z - np.take_along_axis(x, f[:, :, None, :], 3)))
        A = np.count_nonzero(np.logical_not(found), axis=(1, 2)) & 255
        first = np.full((N, 8, W), P, np.int64)
        np.minimum.at(first, (qi, gi, np.concatenate([v, f], axis=2)), np.concatenate([pn, pn])[None, None, :])
        stands = (f != v) & (np.take_along_axis(first, v, 2) == pn) & (np.take_along_axis(first, f, 2) == pn)
        q, g, p = np.nonzero(stands); a = v[q, g, p]; b = f[q, g, p]
        ca = e[q, g, :, a]; cb = e[q, g, :, b]
        na = np.where(k16 % 2 == 0, cb, ca); nb = np.where(k16 % 2 == 0, ca, cb)
        na[:, 15] = b + W * (9 + t); nb[:, 15] = a + W * (9 + t)
        e[q, g, :, a] = na; e[q, g, :, b] = nb
        v = f
    return {"ys": np.add.reduce(e * (k16[:, None] + 1), axis=2).astype(np.float32), "yp": (v + W * tau).astype(np.float32), "yz": z.reshape(N, 128, P).astype(np.float32).astype(BF)}

@@ -1,0 +1,577 @@
+import numpy as np
+from concourse.mybir import AluOpType as A, ActivationFunctionType as F, AxisListType as AX
+
+HOPS = 5
+G1, V1, G0 = 10, 6, 12
+CH = (1, 0)
+RB = ("pb5", "pb7")
+f4, f2, b2, i4, u2 = "float32", "float16", "bfloat16", "int32", "uint16"
+SCRATCH = {}
+OWNBUF = ("enS", "tmpB", "NT", "ST", "XS", "FV", "FF", "NTh", "YS", "YP", "YZ", "v0s", "z0s", "wts", "ZI", "X", "S", "M", "D", "AB", "ZE",
+          "VAL", "VV", "OWN", "MM", "Zz", "MO", "ZO", "RT", "OT", "RL", "AL", "POS", "NNs", "NSs")
+PLACE = {}
+
+
+def declare(name, w, t):
+    if name in OWNBUF:
+        SCRATCH[name] = ("sbuf", [128, w], t)
+        PLACE[name] = (name, 0, w)
+        return
+    pool = "pool" + t
+    a = SCRATCH[pool][1][1] if pool in SCRATCH else 0
+    SCRATCH[pool] = ("sbuf", [128, a + w + w % 2], t)
+    PLACE[name] = (pool, a, w)
+
+
+for n_, w_, t_ in (
+        ("enS", 2048, i4), ("tmpB", 2048, b2), ("NT", 2432, f4), ("ST", 2432, b2), ("XS", 2048, b2),
+        ("FV", 2064, f4), ("FF", 2064, f4), ("NTh", 2048, f2), ("YS", 2048, f4), ("YP", 192, f4), ("YZ", 192, b2),
+        ("v0s", 12, i4), ("v0f", 12, f4), ("z0s", 192, b2), ("wts", 1, i4), ("wtf", 1, f4),
+        ("ones", 192, f2), ("onef", 32, f4), ("o32", 136, f2), ("ID", 128, f2), ("NID", 128, f2), ("P64", 128, f2), ("N64", 128, f2),
+        ("I2K", 128, f2), ("IDb", 128, b2), ("I22", 128, b2), ("INK", 128, b2), ("BDt", 128, f2), ("BD", 128, f2), ("GBt", 8, f4), ("GB", 8, f4), ("GBs", 8, f4), ("GBy", 8, f4),
+        ("BAND", 160, f2), ("ZI", 2560, f2), ("qI", 1, i4), ("qJ", 1, i4), ("qK", 1, i4), ("qi", 1, f4), ("qe", 1, f4), ("q15", 1, f4),
+        ("qo", 1, f4), ("q24", 1, f4), ("qs1", 1, f4), ("TC", 1, f4), ("w1", 1, f4),
+        ("CI", 192, f4), ("RM16", 16, f4), ("WC", 16, f4), ("selB", 128, b2), ("WN", 128, b2), ("SELT", 136, f2),
+        ("W16", 8, b2), ("WD", 8, f2), ("YWn", 8, f2), ("YWs", 8, b2), ("EXPT", 136, f2), ("KTHR", 136, f4), ("BK", 136, b2),
+        ("RST", 136, f4), ("NEG", 192, f4), ("EQD", 192, f4), ("OFFD", 192, f4), ("HOLD", 192, f4), ("SEG", 192, f4), ("TR", 24, f4), ("TRb", 24, f4),
+        ("DO", 128, f2), ("DE", 128, f2), ("D15", 128, f2), ("DOb", 128, b2), ("DEb", 128, b2), ("BT", 5, f4),
+        ("GFt", 128, f2), ("GTt", 128, f2), ("GF", 128, f2), ("GT", 128, f2), ("LM", 192, f2),
+        ("vlf", 12, f4), ("FL", 192, f4), ("CN", 192, f2), ("RL", 192, u2), ("X", 3072, f2), ("S", 3072, b2), ("M", 3072, b2), ("D", 3072, b2), ("AB", 3072, b2), ("ZE", 3072, f2),
+        ("AL", 192, u2), ("TBc", 272, b2), ("ui", 16, i4), ("ua", 16, i4), ("ub", 16, i4), ("uc", 16, i4), ("ud", 16, i4), ("ue", 16, i4), ("uf", 16, i4), ("ff", 16, f2),
+        ("Af", 1, f4), ("Ai", 1, i4), ("Aj", 1, i4), ("Ac", 1, f4), ("FC", 16, f2), ("TPs", 192, f2),
+        ("Rv", 192, f2), ("Sv", 192, b2), ("Rf", 192, f2), ("Sf", 192, b2), ("G0", 192, f4), ("pre", 192, f4),
+        ("ma", 192, f4), ("mb", 192, f4), ("nd", 192, f4), ("ns", 192, f4), ("nT", 24, f4), ("nP", 24, f4), ("POS", 24, u2),
+        ("NNs", 384, f4), ("NSs", 384, b2), ("XF", 192, f2), ("AZ", 192, f2), ("FM", 192, f2), ("R1", 192, f2), ("R2", 192, f2),
+        ("VAL", 960, f4), ("VV", 960, f4), ("OWN", 960, f4),
+        ("MM", 1920, f2), ("Zz", 960, f2), ("MO", 1920, f2), ("ZO", 960, f2), ("RT", 200, u2), ("OT", 200, u2)):
+    declare(n_, w_, t_)
+for c_ in (0, 1):
+    for n_, w_, t_ in (("Mn", 136, f4), ("dd", 136, f4), ("ee", 136, f4), ("oo", 136, f4), ("WT", 16, f2), ("RMk", 96, f4),
+                       ("eq", 96, f4), ("dup", 96, f4), ("pT", 6, f4), ("pQ", 6, f4)):
+        declare(n_ + str(c_), w_, t_)
+for b_ in range(8):
+    SCRATCH["pb%d" % b_] = ("psum", [128, 512], f4)
+    PLACE["pb%d" % b_] = ("pb%d" % b_, 0, 512)
+SEMAPHORES = ["cV", "cS", "cP", "cG", "sent"] + ["ld%d" % k for k in range(8)] + ["st%d" % k for k in range(3)] + \
+    ["a%s%d" % (m, t) for m in ("M", "L", "Z0", "Z1") for t in range(1, HOPS)]
+
+
+def meet(x, y):
+    return x[1] < y[2] and y[1] < x[2] and not (x[3] == y[3] and (x[1] - y[1]) % x[3])
+
+
+def make(g, T):
+    eng = {"V": g.vector, "S": g.scalar, "P": g.tensor, "G": g, "Y": g.sync}
+    cnt = {"V": 0, "S": 0, "P": 0, "G": 0}
+    clk = {q: {} for q in eng}
+    snap, acc = {}, {}
+
+    def semof(r):
+        return T.sem["c" + r] if r in cnt else T.sem[r]
+
+    def B(name, a=None, b=None, step=1, r0=0, r1=128):
+        name, o, w = PLACE[name]
+        a, b = (o, o + w) if a is None else (o + a, o + b)
+        return (T[name][r0:r1, a:b:step] if step != 1 else T[name][r0:r1, a:b], [(name, a, b, step)])
+
+    def I(win, off):
+        return (win[0].indirect(off[0]), win[1] + off[1])
+
+    def learn(q, r, n):
+        c = clk[q]
+        c[r] = max(c.get(r, 0), n)
+        for k, v in snap.get((r, n), {}).items():
+            if c.get(k, 0) < v:
+                c[k] = v
+
+    def sync(q, reads, writes):
+        need = {}
+        for regs, w in ((reads, False), (writes, True)):
+            for reg in regs:
+                ps = reg[0].startswith("pb")
+                for (rq, rn, old, rw) in acc.get(reg[0], ()):
+                    hit = meet(reg, old)
+                    if rq == q:
+                        if q == "P" or not rw or not hit:
+                            continue
+                    elif not (ps or (hit and (w or rw))):
+                        continue
+                    if need.get(rq, 0) < rn:
+                        need[rq] = rn
+        order = sorted(need, key=lambda r: (r not in cnt, -need[r]))
+        for final in (False, True):
+            for r in order:
+                if clk[q].get(r, 0) >= need[r]:
+                    continue
+                if not final and any(o != r and clk[q].get(o, 0) < need[o] and snap[(o, need[o])].get(r, 0) >= need[r] for o in order):
+                    continue
+                eng[q].wait_ge(semof(r), need[r])
+                learn(q, r, need[r])
+
+    def note(ev, n, reads, writes):
+        for reg in writes:
+            acc[reg[0]] = [x for x in acc.get(reg[0], []) if not (x[2][1] >= reg[1] and x[2][2] <= reg[2] and (reg[3] == 1 or (x[2][3] == reg[3] and x[2][1] == reg[1])))] + [(ev, n, reg, True)]
+        for reg in reads:
+            acc[reg[0]] = [x for x in acc.get(reg[0], []) if not (x[0] == ev and not x[3] and x[2] == reg)] + [(ev, n, reg, False)]
+
+    def op(q, fn, outs, ins):
+        reads = [r for i in ins for r in i[1]]
+        writes = [r for o in outs for r in o[1]]
+        sync(q, reads, writes)
+        call = fn()
+        cnt[q] += 1
+        n = cnt[q]
+        call.then_inc(semof(q), 1)
+        snap[(q, n)] = dict(clk[q])
+        snap[(q, n)][q] = n - 1
+        note(q, n, reads, writes)
+
+    def sc(x):
+        return x[0] if isinstance(x, tuple) else x
+
+    def tl(*xs):
+        return [x for x in xs if isinstance(x, tuple)]
+
+    def tt(o, a, b, f): op("V", lambda: eng["V"].tensor_tensor(o[0], a[0], b[0], f), [o], [a, b])
+    def ts(o, a, s1, s2, f0, f1=None):
+        if f1 is None:
+            op("V", lambda: eng["V"].tensor_scalar(o[0], a[0], sc(s1), None, f0), [o], [a] + tl(s1))
+        else:
+            op("V", lambda: eng["V"].tensor_scalar(o[0], a[0], sc(s1), sc(s2), f0, f1), [o], [a] + tl(s1, s2))
+    def cp(o, a): op("V", lambda: eng["V"].tensor_copy(o[0], a[0]), [o], [a])
+    def scat(tab, off, a): op("V", lambda: eng["V"].tensor_copy(tab[0].indirect(off[0]), a[0]), [tab], [a, off])
+    def scan(o, a, b, i, f0, f1): op("V", lambda: eng["V"].tensor_tensor_scan(o[0], a[0], b[0], i, f0, f1), [o], [a, b])
+    def red(o, a): op("V", lambda: eng["V"].tensor_reduce(o[0], a[0], AX.X, A.add), [o], [a])
+    def fill(o, c): op("V", lambda: eng["V"].memset(o[0], c), [o], [])
+    def act(o, a, f=F.Copy, scale=1.0, bias=0.0):
+        op("S", lambda: eng["S"].activation(o[0], a[0], f, bias=sc(bias), scale=sc(scale)), [o], [a] + tl(bias, scale))
+    def mm(o, l, r, st=True, sp=True): op("P", lambda: eng["P"].matmul(o[0], l[0], r[0], st, sp), [o], [l, r])
+    def iota(o, pat, base, cm, whole=False):
+        if whole:
+            op("G", lambda: g.iota(o[0], pat, base, cm), [o], [])
+        else:
+            op("G", lambda: g.iota(o[0], pat, base, cm, allow_small_or_imprecise_dtypes=True), [o], [])
+    def asel(o, a, pat, cop, fv, base, cm): op("G", lambda: g.affine_select(o[0], a[0], pat, cop, fv, base, cm), [o], [a])
+
+    def dma(q, sem, out, in_, outs, ins):
+        reads, writes = [r for i in ins for r in i[1]], [r for o in outs for r in o[1]]
+        sync(q, reads, writes)
+        eng[q].dma_start(out, in_).then_inc(T.sem[sem], 16)
+        snap[(sem, 16)] = dict(clk[q])
+        note(sem, 16, reads, writes)
+
+    def arrive(sem, n, b):
+        snap[(sem, n)] = {}
+        note(sem, n, [], b[1])
+
+    def send(core, dst, topo, o, i, rsem):
+        sync("G", i[1], [])
+        rid, pid = topo.addr(dst, core)
+        g.remote_dma(o[0], i[0], T.sem[rsem], T.sem.sent, pid, rid, topo.mask(core, dst))
+        return len(topo.engines(core, dst))
+
+    return dict(B=B, I=I, tt=tt, ts=ts, cp=cp, scat=scat, scan=scan, red=red, fill=fill, act=act, mm=mm, iota=iota, asel=asel, dma=dma,
+                arrive=arrive, send=send, cnt=cnt)
+
+
+def weave(*lists):
+    lists = [list(x) for x in lists]
+    while any(lists):
+        for x in lists:
+            if x:
+                x.pop(0)()
+
+
+def rank_program(g, core, T, topo):
+    rank = T.rank_of(core)
+    if rank is None:
+        return
+    K = make(g, T)
+    B, I, tt, ts, cp, scat, scan, red, fill, act, mm, iota, asel, dma = (K[k] for k in (
+        "B", "I", "tt", "ts", "cp", "scat", "scan", "red", "fill", "act", "mm", "iota", "asel", "dma"))
+    nxt = T.cores[(rank + 3) % len(T.cores)]
+    prv_eng = len(topo.engines(T.cores[(rank + 1) % len(T.cores)], core))
+
+    def dedupe(c, bank, a, flist, fpos):
+        s = str(c)
+        tt(B("RMk" + s), B(bank, a, a + 96), B("NEG", 0, 96), A.add)
+        scan(B("FL", 96 * c, 96 * c + 96), B("HOLD", 0, 96), B("RMk" + s), 0.0, A.add, A.max)
+        own = B("FL", 96 * c + 15, 96 * c + 96, 16)
+        cp(flist, own)
+        tt(B("eq" + s, 0, 95), B(bank, a + 1, a + 96), B("FL", 96 * c, 96 * c + 95), A.is_equal)
+        scan(B("dup" + s, 0, 95), B("SEG", 0, 95), B("eq" + s, 0, 95), 0.0, A.mult, A.max)
+        ts(B("pT" + s), B("dup" + s, 14, 95, 16), B("TC"), None, A.mult)
+        tt(B("pQ" + s), B("pT" + s), own, A.max)
+        cp(fpos, B("pQ" + s))
+
+    def marks(tab, val, pos, p0, t, c):
+        return [lambda b=b: scat(B(tab), B(pos, p0 + 2 * b, p0 + 2 * b + 1), B(val, 192 * t + 16 * b, 192 * t + 16 * b + 16))
+                for b in range(6 * c + 5, 6 * c - 1, -1)]
+
+    dma("Y", "ld0", T.v0s[:], T.v0[:], [B("v0s")], [])
+    QW = 512
+    for j in range(4):
+        dma("Y", "ld%d" % (3 + j), T.enS[:, j * QW:(j + 1) * QW], T.en[:, j * QW:(j + 1) * QW], [B("enS", j * QW, (j + 1) * QW)], [])
+    dma("S", "ld1", T.z0s[:], T.z0[:], [B("z0s")], [])
+    dma("S", "ld2", T.wts[:], T.wt[:], [B("wts")], [])
+    dma("S", "ld7", T.XS[:], T.xs[:], [B("XS")], [])
+
+    fill(B("ones"), 1.0); fill(B("onef"), 1.0); fill(B("GFt"), 32.0); fill(B("GTt"), 1024.0); fill(B("o32"), 1.0 / 32)
+    iota(B("qI"), [[0, 1]], 0, 1, True)
+    iota(B("CI"), [[0, 12], [1, 16]], 0, 0)
+    asel(B("BDt"), B("ones", 0, 128), [[-16, 8], [0, 16]], A.is_ge, 0.0, 0, 1)
+    asel(B("BD"), B("BDt"), [[16, 8], [0, 16]], A.is_ge, 0.0, 15, -1)
+    asel(B("BAND"), B("ones", 0, 160), [[1, 160]], A.is_equal, 0.0, -16, -1)
+    asel(B("GBt"), B("onef", 0, 8), [[-16, 8]], A.is_ge, 0.0, 0, 1)
+    asel(B("GB"), B("GBt"), [[16, 8]], A.is_ge, 0.0, 15, -1)
+    asel(B("ID"), B("ones", 0, 128), [[-1, 128]], A.is_equal, 0.0, 0, 1)
+    iota(B("VAL", 0, 192), [[32, 12], [-2, 16]], 30, 0)
+    iota(B("VV", 0, 192), [[32, 12], [-2, 16]], 29, 0)
+    asel(B("EXPT"), B("ones", 0, 136), [[-16, 8], [0, 17]], A.is_equal, 0.0, 0, 1)
+    iota(B("FV"), [[0, 2064]], 9999, 0)
+    ts(B("qJ"), B("qI"), 15, None, A.bitwise_and)
+    cp(B("qi"), B("qJ"))
+    ts(B("RM16"), B("CI", 0, 16), B("qi"), None, A.is_equal)
+    ts(B("WC"), B("RM16"), -2097152.0 + 8192.0, -8192.0, A.mult, A.add)
+    act(B("GBs"), B("GB"), scale=2.0 ** -10)
+    for i in range(16):
+        act(B("selB", 8 * i, 8 * i + 8), B("GBs"), scale=B("RM16", i, i + 1))
+        act(B("WN", 8 * i, 8 * i + 8), B("GB"), scale=B("WC", i, i + 1))
+    act(B("INK"), B("ID"), scale=-2048.0)
+    ts(B("EQD"), B("CI"), B("qi"), None, A.is_equal)
+    ts(B("NEG"), B("EQD"), 4096.0, -4096.0, A.mult, A.add)
+    fill(B("HOLD"), 0.0); fill(B("SEG"), 1.0); fill(B("OT"), 0); fill(B("MM", 192, 384), 0.0)
+    fill(B("HOLD", 0, 192, 16), -8192.0); fill(B("SEG", 0, 192, 16), 0.0)
+    cp(B("v0f"), B("v0s"))
+    for i in range(16):
+        act(B("LM", i, 192, 16), B("v0f"), scale=B("RM16", 15 - i, 16 - i))
+    mm(B("pb7", 0, 192), B("BD"), B("LM"))
+    act(B("MM", 0, 192), B("pb7", 0, 192))
+    ts(B("TC"), B("qi"), 2048.0, None, A.add)
+    for i in range(16):
+        ts(B("ZI", 160 * i, 160 * i + 160), B("BAND"), B("RM16", i, i + 1), None, A.mult)
+    fill(B("NT", 2048, 2432), 0.0); fill(B("ST", 2048, 2432), 0.0)
+    for j in range(4):
+        a, b = j * QW, (j + 1) * QW
+        ts(B("tmpB", a, b), B("enS", a, b), 1.0 / 2048, 159.5 + 1.0 / 8192, A.mult, A.add)
+        act(B("ST", a, b), B("tmpB", a, b), bias=-160.0)
+        mm(B("pb%d" % j), B("INK"), B("ST", a, b))
+    for i in range(16):
+        act(B("Zz", i, 192, 16), B("z0s", 15 - i, 192, 16))
+    for c in CH:
+        dedupe(c, "pb7", 96 * c, B("RT", 6 * c, 6 * c + 6), B("RT", 12 + 12 * c, 24 + 12 * c, 2))
+    ts(B("qs1"), B("qi"), 1.0, None, A.add)
+    cp(B("wtf"), B("wts"))
+    ts(B("q15"), B("qi"), 15.0, None, A.is_equal)
+    ts(B("qK"), B("qJ"), 1, None, A.bitwise_and)
+    ts(B("qe"), B("qK"), -1.0, 1.0, A.mult, A.add)
+    tt(B("w1"), B("qe"), B("q15"), A.add)
+    ts(B("qo"), B("w1"), -1.0, 1.0, A.mult, A.add)
+    act(B("W16"), B("GB"), scale=1024.0)
+    act(B("WD"), B("GB"), scale=B("wtf"))
+    act(B("IDb"), B("ID")); act(B("I22"), B("ID"), scale=4194304.0)
+    for j in range(4):
+        a, b = j * QW, (j + 1) * QW
+        tt(B("NT", a, b), B("enS", a, b), B("pb%d" % j), A.add)
+
+    def consts_late(part):
+        if part:
+            iota(B("FF"), [[0, 2064]], 9999, 0)
+            for t in range(1, HOPS):
+                iota(B("VAL", 192 * t, 192 * t + 192), [[32, 12], [-2, 16]], 30 - 512 * t, 0)
+                iota(B("VV", 192 * t, 192 * t + 192), [[32, 12], [-2, 16]], 29 - 512 * t, 0)
+            return
+        asel(B("SELT"), B("o32"), [[-16, 8], [-1, 17]], A.is_equal, 0.0, 1, 1)
+        iota(B("KTHR"), [[0, 8], [-1, 17]], 17, 0)
+        iota(B("BK"), [[0, 8], [64, 17]], -64, 0)
+        asel(B("GF", 0, 128, 1, 0, 16), B("GFt", 0, 128, 1, 0, 16), [[-1, 8], [0, 16]], A.is_equal, 0.0, 0, 1)
+        asel(B("GT", 0, 128, 1, 0, 16), B("GTt", 0, 128, 1, 0, 16), [[-1, 8], [0, 16]], A.is_equal, 0.0, -8, 1)
+        iota(B("TRb"), [[1, 24]], 2048, 0)
+
+    def consts_v1():
+        return [lambda: fill(B("SELT", 0, 136, 17), 0.0), lambda: fill(B("BK", 0, 136, 17), -524288.0),
+                lambda: fill(B("RST"), -1.0e7), lambda: fill(B("RST", 0, 136, 17), 1.0e7)]
+
+    def consts_v2():
+        return [lambda: ts(B("q24"), B("qi"), 24.0, None, A.mult), lambda: ts(B("TR"), B("TRb"), B("q24"), None, A.add),
+                lambda: ts(B("OFFD"), B("EQD"), 1.0e6, -1.0e6, A.mult, A.add),
+                lambda: tt(B("OWN", 0, 192), B("VAL", 0, 192), B("OFFD"), A.add)]
+
+    def consts_s():
+        act(B("NID"), B("ID"), scale=-1.0); act(B("P64"), B("ID"), scale=64.0); act(B("N64"), B("ID"), scale=-64.0)
+        act(B("DE"), B("ID"), scale=B("qe")); act(B("DO"), B("ID"), scale=B("qo")); act(B("D15"), B("ID"), scale=B("q15"))
+        act(B("DEb"), B("ID"), scale=B("qe")); act(B("DOb"), B("ID"), scale=B("qo"))
+        for t in range(HOPS):
+            act(B("BT", t, t + 1), B("q15"), scale=9.0 + t)
+        act(B("I2K"), B("ID"), scale=2048.0)
+        act(B("GBy"), B("GB"), scale=2048.0)
+        act(B("YWn"), B("GB"), scale=B("qs1")); act(B("YWs"), B("GBy"), scale=B("qs1"))
+
+    sent = 0
+    held = []
+    for t in range(HOPS):
+        last = t == HOPS - 1
+        zc, mc, rc = 192 * t, 384 * t, 40 * t
+        if t > 0:
+            K["arrive"]("aL%d" % t, prv_eng, B("RT", rc, rc + 36))
+            K["arrive"]("aM%d" % t, prv_eng, B("MM", mc, mc + 384))
+            for c in CH:
+                K["arrive"]("aZ%d%d" % (c, t), prv_eng, B("Zz", zc + 96 * c, zc + 96 * c + 96))
+        vl, fl = B("RT", rc, rc + 12), B("OT", rc, rc + 12)
+
+        def W(n, a=0, b=16, st=1):
+            return B(n, a, b, st, 0, 96)
+
+        def bc(name, c, k):
+            return B(name, 1536 * c + k, 1536 * c + 1536, 16)
+
+        def gat(c, what):
+            act(B(what, 1536 * c, 1536 * c + 1536), I(B("NT" if what == "X" else "ST"), B("RL", 96 * c, 96 * c + 96)))
+
+        def selx(c):
+            for k in range(16):
+                i = (k + t) % 16
+                off = 160 * i + 16 - (k - i)
+                mm(B("pb4", 96 * c, 96 * c + 96), B("ZI", off, off + 128), bc("X", c, k), k == 0, k == 15)
+
+        def lists(c):
+            cp(B("AL", 96 * c, 96 * c + 96), B("pb4", 96 * c, 96 * c + 96))
+            cp(B("CN", 96 * c, 96 * c + 96), B("AL", 96 * c, 96 * c + 96))
+
+        def rec(c):
+            tt(B("D", 1536 * c, 1536 * c + 1536), I(B("XS"), B("AL", 96 * c, 96 * c + 96)), B("ZE", 1536 * c, 1536 * c + 1536), A.subtract)
+
+        def size(c):
+            act(B("AB", 1536 * c, 1536 * c + 1536), B("D", 1536 * c, 1536 * c + 1536), F.Abs)
+
+        def newer(c):
+            for k in range(16):
+                tt(bc("M", c, k), bc("S", c, k), B("pb5", 96 * c, 96 * c + 96), A.is_gt)
+
+        def pay(c):
+            mm(W("pb%d" % (2 + c), 0, 136), B("CN", 96 * c, 96 * c + 96), B("SELT"), True, False)
+            for k in range(16):
+                i = (k + t) % 16
+                mm(W("pb%d" % (2 + c), 1 + k, 136, 17), bc("S", c, k), B("selB", 8 * i, 8 * i + 8), False, False)
+
+        def failcol(c):
+            mm(W("pb%d" % (2 + c), 0, 136, 17), W("ID", 0, 96), W("ff", 8 * c, 8 * c + 8), False, True)
+
+        def key0(c):
+            mm(W("pb%d" % c, 0, 136), W("IDb", 0, 96), W("BK", 0, 136), True, False)
+            mm(W("pb%d" % c, 0, 136), W("I22", 0, 96), W("TBc", 136 * c, 136 * c + 136), False, False)
+
+        def keyA(c):
+            for k in range(16):
+                mm(W("pb%d" % c, 1 + k, 136, 17), bc("AB", c, k), B("W16"), False, False)
+
+        def keyM(c):
+            for k in range(16):
+                i = (k + t) % 16
+                mm(W("pb%d" % c, 1 + k, 136, 17), bc("M", c, k), B("WN", 8 * i, 8 * i + 8), False, k == 15)
+
+        def zexp(c, q, k0, k1):
+            for k in range(k0, k1):
+                z = B("Zz", zc + 96 * c, zc + 96 * c + 96)
+                if q == "G":
+                    asel(bc("ZE", c, k), z, [[0, 96]], A.is_equal, 0.0, 0, 0)
+                elif q == "S":
+                    act(bc("ZE", c, k), z)
+                else:
+                    cp(bc("ZE", c, k), z)
+
+        def tail(c):
+            s = str(c)
+            kk, pp = W("pb%d" % c, 0, 136), W("pb%d" % (2 + c), 0, 136)
+            mn, dd, ee, oo = (W(n + s, 0, 136) for n in ("Mn", "dd", "ee", "oo"))
+            scan(mn, W("RST", 0, 136), kk, 0.0, A.max, A.min)
+            tt(dd, kk, mn, A.subtract)
+            tt(ee, pp, dd, A.subtract)
+            scan(oo, dd, ee, 0.0, A.min, A.max)
+            o16 = W("oo" + s, 16, 136, 17)
+            ts(W("WT" + s, 0, 8), o16, 393216.0, 393216.0, A.add, A.subtract)
+            tt(W("WT" + s, 8, 16), o16, W("WT" + s, 0, 8), A.subtract)
+
+        def turn(c):
+            q = B("pb6", 320 + 96 * c, 416 + 96 * c, 1, 0, 16)
+            tp = B("TPs", 96 * c, 96 * c + 96, 1, 0, 16)
+            mm(q, W("WT%d" % c, 0, 16), W("ID", 0, 96))
+            act(tp, q)
+            mm(B(RB[c], 0, 96), B("GF", 0, 128, 1, 0, 16), tp)
+            mm(B(RB[c], 96, 192), B("GT", 0, 128, 1, 0, 16), tp)
+
+        def share(c):
+            for k in (0, 1):
+                act(B("MO", mc + 192 * k + 96 * c, mc + 192 * k + 96 * c + 96), B(RB[c], 96 * k, 96 * k + 96))
+
+        def zproc(c):
+            a, b = 96 * c, 96 * c + 96
+            zt = B("Zz", zc + a, zc + b)
+            act(B("FM", a, b), B(RB[c], 96, 192), F.Relu, scale=-1.0, bias=1.0)
+            act(B("XF", a, b), I(B("XS"), B("OT", rc + 6 * c, rc + 6 * c + 6)))
+            mm(B("pb1", a, b), B("ID"), zt, True, False)
+            mm(B("pb1", a, b), B("NID"), B("XF", a, b), False, True)
+            mm(B("pb3", a, b), B("ID"), zt, True, False)
+            mm(B("pb3", a, b), B("N64"), B("FM", a, b), False, True)
+            act(B("AZ", a, b), B("pb1", a, b), F.Abs)
+            act(B("R1", a, b), B("pb3", a, b), F.Relu)
+            mm(B("pb3", 192 + a, 192 + b), B("ID"), B("AZ", a, b), True, False)
+            mm(B("pb3", 192 + a, 192 + b), B("P64"), B("FM", a, b), False, True)
+            act(B("R2", a, b), B("pb3", 192 + a, 192 + b), F.Relu, bias=-64.0)
+            mm(B("pb1", 192 + a, 192 + b), B("ID"), B("R1", a, b), True, False)
+            mm(B("pb1", 192 + a, 192 + b), B("ID"), B("R2", a, b), False, True)
+            if not last:
+                act(B("ZO", zc + a, zc + b), B("pb1", 192 + a, 192 + b))
+
+        def out(o, src, n, a, b, sem):
+            if last:
+                return 0
+            return K["send"](core, nxt, topo, B(o, n * (t + 1) + a, n * (t + 1) + b), B(src, n * t + a, n * t + b), sem + str(t + 1))
+
+        for c in CH:
+            cp(B("RL", 96 * c, 96 * c + 96), I(B("NT"), B("RT", rc + 6 * c, rc + 6 * c + 6)))
+        gat(1, "X")
+        for f_ in held:
+            f_()
+        zexp(1, "S", G1 + V1, 16)
+        gat(1, "S"); gat(0, "X")
+        zexp(0, "S", G0, 16)
+        mm(B("pb5", 0, 192), B("ID"), B("MM", mc + 192, mc + 384))
+        for c in (0, 1):
+            mm(W("pb6", 136 * c, 136 * c + 136), B("MM", mc + 192 + 96 * c, mc + 288 + 96 * c), B("EXPT"))
+        selx(1)
+        zexp(1, "G", 0, G1)
+        if t == 0:
+            consts_late(0)
+        zexp(0, "G", 0, G0)
+        if t == 0:
+            consts_late(1)
+        e1, e2 = [], []
+        for c in (0, 1):
+            e1.append(lambda c=c: tt(W("TBc", 136 * c, 136 * c + 136), W("pb6", 136 * c, 136 * c + 136), W("KTHR", 0, 136), A.is_ge))
+        e1.append(lambda: cp(B("vlf"), vl))
+        if t > 0:
+            e1.append(lambda: red(W("Af", 0, 1), W("pb3", 480, 496)))
+            e1.append(lambda: cp(W("Ai", 0, 1), W("Af", 0, 1)))
+            e1.append(lambda: ts(W("Aj", 0, 1), W("Ai", 0, 1), 255, None, A.bitwise_and))
+            e1.append(lambda: cp(W("Ac", 0, 1), W("Aj", 0, 1)))
+        else:
+            e1.append(lambda: fill(B("Ac"), 0.0))
+        e2.append(lambda: cp(W("ui"), W("pb6", 288, 304)))
+        e2.append(lambda: ts(W("ua"), W("ui"), 2047, None, A.bitwise_and))
+        e2.append(lambda: tt(W("ub"), W("ua"), W("ua"), A.mult))
+        e2.append(lambda: ts(W("ud"), W("ua"), 37.0, W("Ac", 0, 1), A.mult, A.add))
+        e2.append(lambda: ts(W("uc"), W("ub"), 5, None, A.arith_shift_right))
+        e2.append(lambda: tt(W("ue"), W("uc"), W("ud"), A.add))
+        e2.append(lambda: ts(W("uf"), W("ue"), 2047, None, A.bitwise_and))
+        e2.append(lambda: ts(W("ff"), W("uf"), 1.0 / 32, None, A.mult))
+        sv = marks("FV", "VV", "RT", rc + 12, t, 1) + marks("FV", "VV", "RT", rc + 12, t, 0)
+        weave(sv, e1, consts_v1() if t == 0 else [])
+        zexp(1, "V", G1, G1 + V1)
+        lists(1); rec(1)
+        size(1)
+        gat(0, "S")
+        pay(1)
+        newer(1)
+        selx(0)
+        key0(1); keyA(1); keyM(1)
+        for c in (0, 1):
+            mm(W("pb6", 288 + 8 * c, 296 + 8 * c), B("Zz", zc + 96 * c, zc + 96 * c + 96), B("WD"))
+        lists(0); rec(0)
+        pay(0); key0(0)
+        weave(e2, consts_v2() if t == 0 else [])
+        failcol(1); failcol(0)
+        size(0)
+        keyA(0)
+        tail(1)
+        turn(1)
+        newer(0)
+        act(B("Rv"), I(B("NT"), vl))
+        act(B("Sv"), I(B("ST"), vl))
+        act(B("G0"), I(B("FV"), vl), bias=1.0)
+        if t > 0:
+            act(B("OWN", zc, zc + 192), B("OWN", 0, 192), bias=-512.0 * t)
+        else:
+            consts_s()
+        share(1)
+        keyM(0)
+        tail(0)
+        dedupe(1, RB[1], 0, B("OT", rc + 6, rc + 12), B("OT", rc + 24, rc + 36, 2))
+        turn(0)
+        share(0)
+        zproc(1)
+        sent += out("Zz", "ZO", 192, 96, 192, "aZ1")
+        weave(marks("FF", "VAL", "OT", rc + 12, t, 1), [lambda c=c: ts(W("FC", 8 * c, 8 * c + 8), W("WT%d" % c, 8, 16), 0.0, None, A.is_equal) for c in (0, 1)])
+        dedupe(0, RB[0], 0, B("OT", rc, rc + 6), B("OT", rc + 12, rc + 24, 2))
+        sent += out("MM", "MO", 384, 0, 384, "aM")
+        sent += out("RT", "OT", 40, 0, 36, "aL")
+        act(B("Rf"), I(B("NT"), fl))
+        act(B("Sf"), I(B("ST"), fl))
+        weave(marks("FF", "VAL", "OT", rc + 12, t, 0), [lambda: tt(B("pre"), I(B("FV"), fl), B("G0"), A.min)])
+        vr, fr = B("MM", mc, mc + 192), B("MO", mc, mc + 192)
+        for h, (own, oth, new) in enumerate((("Rv", "Rf", fr), ("Rf", "Rv", vr))):
+            o = B("pb0", 192 * h, 192 * h + 192)
+            mm(o, B("DO"), B(own), True, False)
+            mm(o, B("D15"), new, False, False)
+            mm(o, B("DE"), B(oth), False, True)
+        act(B("NNs"), B("pb0", 0, 384))
+        for h, (own, oth) in enumerate((("Sv", "Sf"), ("Sf", "Sv"))):
+            o = B("pb2", 192 * h, 192 * h + 192)
+            mm(o, B("DOb"), B(own), True, False)
+            mm(o, B("DEb"), B(oth), False, True)
+        act(B("NSs"), B("pb2", 0, 384), F.Identity, bias=B("BT", t, t + 1))
+        tt(B("ma"), I(B("FF"), vl), B("pre"), A.min)
+        tt(B("mb"), I(B("FF"), fl), B("ma"), A.min)
+        tt(B("nd"), B("mb"), B("OWN", zc, zc + 192), A.is_lt)
+        scan(B("ns"), B("SEG"), B("nd"), 0.0, A.mult, A.max)
+        nl = B("ns", 15, 192, 16)
+        tt(B("nT", 0, 12), nl, B("TR", 0, 12), A.mult)
+        tt(B("nT", 12, 24), nl, B("TR", 12, 24), A.mult)
+        tt(B("nP", 0, 12), B("nT", 0, 12), B("vlf"), A.max)
+        tt(B("nP", 12, 24), B("nT", 12, 24), B("FL", 15, 192, 16), A.max)
+        cp(B("POS"), B("nP"))
+        held = [lambda: scat(B("ST"), B("POS"), B("NSs"))]
+        if last:
+            held[0]()
+        scat(B("NT"), B("POS"), B("NNs"))
+        zproc(0)
+        if not last:
+            sent += out("Zz", "ZO", 192, 0, 96, "aZ0")
+            mm(W("pb3", 480, 496), W("ones", 0, 96), W("FC"))
+
+    mc = 384 * (HOPS - 1)
+    mm(B("pb7", 256, 448), B("ID"), B("MO", mc, mc + 192), True, False)
+    mm(B("pb7", 256, 448), B("I2K"), B("MO", mc + 192, mc + 384), False, True)
+    YB = ("pb2", "pb5", "pb4", "pb0")
+    for j in range(4):
+        mm(B(YB[j], 0, 512, 1, 0, 8), B("YWs"), B("ST", 512 * j, 512 * j + 512), True, False)
+    for i in range(16):
+        act(B("YP", 15 - i, 192, 16), B("pb7", 256 + i, 448, 16))
+    dma("Y", "st1", T.yp[:], T.YP[0:128:16, :], [], [B("YP")])
+    for j in range(4):
+        a, b = 512 * j, 512 * j + 512
+        if j % 2:
+            act(B("NTh", a, b), B("NT", a, b))
+        else:
+            cp(B("NTh", a, b), B("NT", a, b))
+    for j in range(4):
+        mm(B(YB[j], 0, 512, 1, 0, 8), B("YWn"), B("NTh", 512 * j, 512 * j + 512), False, True)
+    for j in range(4):
+        a, b = 512 * j, 512 * j + 512
+        o = B(YB[j], 0, 512, 1, 0, 8)
+        if j % 2:
+            act(B("YS", a, b, 1, 0, 8), o)
+        else:
+            cp(B("YS", a, b, 1, 0, 8), o)
+    dma("Y", "st2", T.ys[:], T.YS[0:8, :], [], [B("YS")])
+    for i in range(16):
+        act(B("YZ", 15 - i, 192, 16), B("pb1", 192 + i, 384, 16))
+    dma("Y", "st0", T.yz[:], T.YZ[:], [], [B("YZ")])
+
+    for q in ("V", "S", "P", "G"):
+        g.wait_ge(T.sem["c" + q], K["cnt"][q])
+    for j in range(8):
+        g.wait_ge(T.sem["ld%d" % j], 16)
+    for j in range(3):
+        g.wait_ge(T.sem["st%d" % j], 16)
+    g.wait_ge(T.sem.sent, sent)

@@ -2,7 +2,9 @@ import numpy as np
 from concourse.mybir import AluOpType as A, ActivationFunctionType as F, AxisListType as AX
 
 HOPS = 5
-G1, V1, G0 = 10, 6, 12
+HR = 128
+HX = 1536 + 16 * (HR - 96)
+G1, V1, G0 = 8, 8, 12
 CH = (1, 0)
 RB = ("pb5", "pb7")
 f4, f2, b2, i4, u2 = "float32", "float16", "bfloat16", "int32", "uint16"
@@ -194,15 +196,15 @@ def rank_program(g, core, T, topo):
 
     def dedupe(c, bank, a, flist, fpos):
         s = str(c)
-        tt(B("RMk" + s), B(bank, a, a + 96), B("NEG", 0, 96), A.add)
-        scan(B("FL", 96 * c, 96 * c + 96), B("HOLD", 0, 96), B("RMk" + s), 0.0, A.add, A.max)
         own = B("FL", 96 * c + 15, 96 * c + 96, 16)
-        cp(flist, own)
-        tt(B("eq" + s, 0, 95), B(bank, a + 1, a + 96), B("FL", 96 * c, 96 * c + 95), A.is_equal)
-        scan(B("dup" + s, 0, 95), B("SEG", 0, 95), B("eq" + s, 0, 95), 0.0, A.mult, A.max)
-        ts(B("pT" + s), B("dup" + s, 14, 95, 16), B("TC"), None, A.mult)
-        tt(B("pQ" + s), B("pT" + s), own, A.max)
-        cp(fpos, B("pQ" + s))
+        return [lambda: tt(B("RMk" + s), B(bank, a, a + 96), B("NEG", 0, 96), A.add),
+                lambda: scan(B("FL", 96 * c, 96 * c + 96), B("HOLD", 0, 96), B("RMk" + s), 0.0, A.add, A.max),
+                lambda: tt(B("eq" + s, 0, 95), B(bank, a + 1, a + 96), B("FL", 96 * c, 96 * c + 95), A.is_equal),
+                lambda: cp(flist, own),
+                lambda: scan(B("dup" + s, 0, 95), B("SEG", 0, 95), B("eq" + s, 0, 95), 0.0, A.mult, A.max),
+                lambda: ts(B("pT" + s), B("dup" + s, 14, 95, 16), B("TC"), None, A.mult),
+                lambda: tt(B("pQ" + s), B("pT" + s), own, A.max),
+                lambda: cp(fpos, B("pQ" + s))]
 
     def marks(tab, val, pos, p0, t, c):
         return [lambda b=b: scat(B(tab), B(pos, p0 + 2 * b, p0 + 2 * b + 1), B(val, 192 * t + 16 * b, 192 * t + 16 * b + 16))
@@ -258,8 +260,7 @@ def rank_program(g, core, T, topo):
         mm(B("pb%d" % j), B("INK"), B("ST", a, b))
     for i in range(16):
         act(B("Zz", i, 192, 16), B("z0s", 15 - i, 192, 16))
-    for c in CH:
-        dedupe(c, "pb7", 96 * c, B("RT", 6 * c, 6 * c + 6), B("RT", 12 + 12 * c, 24 + 12 * c, 2))
+    weave(*[dedupe(c, "pb7", 96 * c, B("RT", 6 * c, 6 * c + 6), B("RT", 12 + 12 * c, 24 + 12 * c, 2)) for c in CH])
     ts(B("qs1"), B("qi"), 1.0, None, A.add)
     cp(B("wtf"), B("wts"))
     ts(B("q15"), B("qi"), 15.0, None, A.is_equal)
@@ -345,8 +346,7 @@ def rank_program(g, core, T, topo):
             act(B("AB", 1536 * c, 1536 * c + 1536), B("D", 1536 * c, 1536 * c + 1536), F.Abs)
 
         def newer(c):
-            for k in range(16):
-                tt(bc("M", c, k), bc("S", c, k), B("pb5", 96 * c, 96 * c + 96), A.is_gt)
+            return [lambda k=k: tt(bc("M", c, k), bc("S", c, k), B("pb5", 96 * c, 96 * c + 96), A.is_gt) for k in range(16)]
 
         def pay(c):
             mm(W("pb%d" % (2 + c), 0, 136), B("CN", 96 * c, 96 * c + 96), B("SELT"), True, False)
@@ -384,13 +384,11 @@ def rank_program(g, core, T, topo):
             s = str(c)
             kk, pp = W("pb%d" % c, 0, 136), W("pb%d" % (2 + c), 0, 136)
             mn, dd, ee, oo = (W(n + s, 0, 136) for n in ("Mn", "dd", "ee", "oo"))
-            scan(mn, W("RST", 0, 136), kk, 0.0, A.max, A.min)
-            tt(dd, kk, mn, A.subtract)
-            tt(ee, pp, dd, A.subtract)
-            scan(oo, dd, ee, 0.0, A.min, A.max)
             o16 = W("oo" + s, 16, 136, 17)
-            ts(W("WT" + s, 0, 8), o16, 393216.0, 393216.0, A.add, A.subtract)
-            tt(W("WT" + s, 8, 16), o16, W("WT" + s, 0, 8), A.subtract)
+            return [lambda: scan(mn, W("RST", 0, 136), kk, 0.0, A.max, A.min), lambda: tt(dd, kk, mn, A.subtract),
+                    lambda: tt(ee, pp, dd, A.subtract), lambda: scan(oo, dd, ee, 0.0, A.min, A.max),
+                    lambda: ts(W("WT" + s, 0, 8), o16, 393216.0, 393216.0, A.add, A.subtract),
+                    lambda: tt(W("WT" + s, 8, 16), o16, W("WT" + s, 0, 8), A.subtract)]
 
         def turn(c):
             q = B("pb6", 320 + 96 * c, 416 + 96 * c, 1, 0, 16)
@@ -430,11 +428,12 @@ def rank_program(g, core, T, topo):
 
         for c in CH:
             cp(B("RL", 96 * c, 96 * c + 96), I(B("NT"), B("RT", rc + 6 * c, rc + 6 * c + 6)))
-        gat(1, "X")
+        act(B("X", 1536, HX), I(B("NT"), B("RL", 96, HR)))
+        cp(B("X", HX, 3072), I(B("NT"), B("RL", HR, 192)))
         for f_ in held:
             f_()
         zexp(1, "S", G1 + V1, 16)
-        gat(1, "S"); gat(0, "X")
+        gat(0, "X"); gat(1, "S")
         zexp(0, "S", G0, 16)
         mm(B("pb5", 0, 192), B("ID"), B("MM", mc + 192, mc + 384))
         for c in (0, 1):
@@ -465,44 +464,44 @@ def rank_program(g, core, T, topo):
         e2.append(lambda: tt(W("ue"), W("uc"), W("ud"), A.add))
         e2.append(lambda: ts(W("uf"), W("ue"), 2047, None, A.bitwise_and))
         e2.append(lambda: ts(W("ff"), W("uf"), 1.0 / 32, None, A.mult))
-        sv = marks("FV", "VV", "RT", rc + 12, t, 1) + marks("FV", "VV", "RT", rc + 12, t, 0)
-        weave(sv, e1, consts_v1() if t == 0 else [])
-        zexp(1, "V", G1, G1 + V1)
+        weave([lambda k=k: zexp(1, "V", k, k + 1) for k in range(G1, G1 + V1)], consts_v1() if t == 0 else [])
         lists(1); rec(1)
         size(1)
         gat(0, "S")
         pay(1)
-        newer(1)
-        selx(0)
-        key0(1); keyA(1); keyM(1)
+        n1 = newer(1)
+        weave(n1[:8], e1)
         for c in (0, 1):
             mm(W("pb6", 288 + 8 * c, 296 + 8 * c), B("Zz", zc + 96 * c, zc + 96 * c + 96), B("WD"))
+        weave(n1[8:], e2)
+        selx(0)
+        key0(1); keyA(1); keyM(1)
+        failcol(1)
         lists(0); rec(0)
-        pay(0); key0(0)
-        weave(e2, consts_v2() if t == 0 else [])
-        failcol(1); failcol(0)
+        pay(0); key0(0); failcol(0)
+        weave(consts_v2() if t == 0 else [])
         size(0)
-        keyA(0)
-        tail(1)
+        n0 = newer(0)
+        weave(n0[:6], tail(1))
         turn(1)
-        newer(0)
+        weave(n0[6:], marks("FV", "VV", "RT", rc + 12, t, 1) + marks("FV", "VV", "RT", rc + 12, t, 0))
+        keyA(0); keyM(0)
         act(B("Rv"), I(B("NT"), vl))
         act(B("Sv"), I(B("ST"), vl))
-        act(B("G0"), I(B("FV"), vl), bias=1.0)
         if t > 0:
             act(B("OWN", zc, zc + 192), B("OWN", 0, 192), bias=-512.0 * t)
         else:
             consts_s()
         share(1)
-        keyM(0)
-        tail(0)
-        dedupe(1, RB[1], 0, B("OT", rc + 6, rc + 12), B("OT", rc + 24, rc + 36, 2))
+        act(B("G0"), I(B("FV"), vl), bias=1.0)
+        weave(tail(0), dedupe(1, RB[1], 0, B("OT", rc + 6, rc + 12), B("OT", rc + 24, rc + 36, 2)))
         turn(0)
         share(0)
         zproc(1)
         sent += out("Zz", "ZO", 192, 96, 192, "aZ1")
-        weave(marks("FF", "VAL", "OT", rc + 12, t, 1), [lambda c=c: ts(W("FC", 8 * c, 8 * c + 8), W("WT%d" % c, 8, 16), 0.0, None, A.is_equal) for c in (0, 1)])
-        dedupe(0, RB[0], 0, B("OT", rc, rc + 6), B("OT", rc + 12, rc + 24, 2))
+        m1 = marks("FF", "VAL", "OT", rc + 12, t, 1)
+        weave(m1[:3], [lambda c=c: ts(W("FC", 8 * c, 8 * c + 8), W("WT%d" % c, 8, 16), 0.0, None, A.is_equal) for c in (0, 1)])
+        weave(dedupe(0, RB[0], 0, B("OT", rc, rc + 6), B("OT", rc + 12, rc + 24, 2)), m1[3:])
         sent += out("MM", "MO", 384, 0, 384, "aM")
         sent += out("RT", "OT", 40, 0, 36, "aL")
         act(B("Rf"), I(B("NT"), fl))

import numpy as np
from concourse.mybir import AluOpType as A, ActivationFunctionType as F, AxisListType as AX

HOPS = 5
HR = 128
HX = 1536 + 16 * (HR - 96)
G1, V1, G0 = 8, 8, 12
CH = (1, 0)
RB = ("pb5", "pb7")
f4, f2, b2, i4, u2 = "float32", "float16", "bfloat16", "int32", "uint16"
SCRATCH = {}
OWNBUF = ("enS", "tmpB", "NT", "ST", "XS", "FV", "FF", "NTh", "YS", "YP", "YZ", "v0s", "z0s", "wts", "ZI", "X", "S", "M", "D", "AB", "ZE",
          "VAL", "VV", "OWN", "MM", "Zz", "MO", "ZO", "RT", "OT", "RL", "AL", "POS", "NNs", "NSs")
PLACE = {}


def declare(name, w, t):
    if name in OWNBUF:
        SCRATCH[name] = ("sbuf", [128, w], t)
        PLACE[name] = (name, 0, w)
        return
    pool = "pool" + t
    a = SCRATCH[pool][1][1] if pool in SCRATCH else 0
    SCRATCH[pool] = ("sbuf", [128, a + w + w % 2], t)
    PLACE[name] = (pool, a, w)


for n_, w_, t_ in (
        ("enS", 2048, i4), ("tmpB", 2048, b2), ("NT", 2432, f4), ("ST", 2432, b2), ("XS", 2048, b2),
        ("FV", 2064, f4), ("FF", 2064, f4), ("NTh", 2048, f2), ("YS", 2048, f4), ("YP", 192, f4), ("YZ", 192, b2),
        ("v0s", 12, i4), ("v0f", 12, f4), ("z0s", 192, b2), ("wts", 1, i4), ("wtf", 1, f4),
        ("ones", 192, f2), ("onef", 32, f4), ("o32", 136, f2), ("ID", 128, f2), ("NID", 128, f2), ("P64", 128, f2), ("N64", 128, f2),
        ("I2K", 128, f2), ("IDb", 128, b2), ("I22", 128, b2), ("INK", 128, b2), ("BDt", 128, f2), ("BD", 128, f2), ("GBt", 8, f4), ("GB", 8, f4), ("GBs", 8, f4), ("GBy", 8, f4),
        ("BAND", 160, f2), ("ZI", 2560, f2), ("qI", 1, i4), ("qJ", 1, i4), ("qK", 1, i4), ("qi", 1, f4), ("qe", 1, f4), ("q15", 1, f4),
        ("qo", 1, f4), ("q24", 1, f4), ("qs1", 1, f4), ("TC", 1, f4), ("w1", 1, f4),
        ("CI", 192, f4), ("RM16", 16, f4), ("WC", 16, f4), ("selB", 128, b2), ("WN", 128, b2), ("SELT", 136, f2),
        ("W16", 8, b2), ("WD", 8, f2), ("YWn", 8, f2), ("YWs", 8, b2), ("EXPT", 136, f2), ("KTHR", 136, f4), ("BK", 136, b2),
        ("RST", 136, f4), ("NEG", 192, f4), ("EQD", 192, f4), ("OFFD", 192, f4), ("HOLD", 192, f4), ("SEG", 192, f4), ("TR", 24, f4), ("TRb", 24, f4),
        ("DO", 128, f2), ("DE", 128, f2), ("D15", 128, f2), ("DOb", 128, b2), ("DEb", 128, b2), ("BT", 5, f4),
        ("GFt", 128, f2), ("GTt", 128, f2), ("GF", 128, f2), ("GT", 128, f2), ("LM", 192, f2),
        ("vlf", 12, f4), ("FL", 192, f4), ("CN", 192, f2), ("RL", 192, u2), ("X", 3072, f2), ("S", 3072, b2), ("M", 3072, b2), ("D", 3072, b2), ("AB", 3072, b2), ("ZE", 3072, f2),
        ("AL", 192, u2), ("TBc", 272, b2), ("ui", 16, i4), ("ua", 16, i4), ("ub", 16, i4), ("uc", 16, i4), ("ud", 16, i4), ("ue", 16, i4), ("uf", 16, i4), ("ff", 16, f2),
        ("Af", 1, f4), ("Ai", 1, i4), ("Aj", 1, i4), ("Ac", 1, f4), ("FC", 16, f2), ("TPs", 192, f2),
        ("Rv", 192, f2), ("Sv", 192, b2), ("Rf", 192, f2), ("Sf", 192, b2), ("G0", 192, f4), ("pre", 192, f4),
        ("ma", 192, f4), ("mb", 192, f4), ("nd", 192, f4), ("ns", 192, f4), ("nT", 24, f4), ("nP", 24, f4), ("POS", 24, u2),
        ("NNs", 384, f4), ("NSs", 384, b2), ("XF", 192, f2), ("AZ", 192, f2), ("FM", 192, f2), ("R1", 192, f2), ("R2", 192, f2),
        ("VAL", 960, f4), ("VV", 960, f4), ("OWN", 960, f4),
        ("MM", 1920, f2), ("Zz", 960, f2), ("MO", 1920, f2), ("ZO", 960, f2), ("RT", 200, u2), ("OT", 200, u2)):
    declare(n_, w_, t_)
for c_ in (0, 1):
    for n_, w_, t_ in (("Mn", 136, f4), ("dd", 136, f4), ("ee", 136, f4), ("oo", 136, f4), ("WT", 16, f2), ("RMk", 96, f4),
                       ("eq", 96, f4), ("dup", 96, f4), ("pT", 6, f4), ("pQ", 6, f4)):
        declare(n_ + str(c_), w_, t_)
for b_ in range(8):
    SCRATCH["pb%d" % b_] = ("psum", [128, 512], f4)
    PLACE["pb%d" % b_] = ("pb%d" % b_, 0, 512)
SEMAPHORES = ["cV", "cS", "cP", "cG", "sent"] + ["ld%d" % k for k in range(8)] + ["st%d" % k for k in range(3)] + \
    ["a%s%d" % (m, t) for m in ("M", "L", "Z0", "Z1") for t in range(1, HOPS)]


def meet(x, y):
    return x[1] < y[2] and y[1] < x[2] and not (x[3] == y[3] and (x[1] - y[1]) % x[3])


def make(g, T):
    eng = {"V": g.vector, "S": g.scalar, "P": g.tensor, "G": g, "Y": g.sync}
    cnt = {"V": 0, "S": 0, "P": 0, "G": 0}
    clk = {q: {} for q in eng}
    snap, acc = {}, {}

    def semof(r):
        return T.sem["c" + r] if r in cnt else T.sem[r]

    def B(name, a=None, b=None, step=1, r0=0, r1=128):
        name, o, w = PLACE[name]
        a, b = (o, o + w) if a is None else (o + a, o + b)
        return (T[name][r0:r1, a:b:step] if step != 1 else T[name][r0:r1, a:b], [(name, a, b, step)])

    def I(win, off):
        return (win[0].indirect(off[0]), win[1] + off[1])

    def learn(q, r, n):
        c = clk[q]
        c[r] = max(c.get(r, 0), n)
        for k, v in snap.get((r, n), {}).items():
            if c.get(k, 0) < v:
                c[k] = v

    def sync(q, reads, writes):
        need = {}
        for regs, w in ((reads, False), (writes, True)):
            for reg in regs:
                ps = reg[0].startswith("pb")
                for (rq, rn, old, rw) in acc.get(reg[0], ()):
                    hit = meet(reg, old)
                    if rq == q:
                        if q == "P" or not rw or not hit:
                            continue
                    elif not (ps or (hit and (w or rw))):
                        continue
                    if need.get(rq, 0) < rn:
                        need[rq] = rn
        order = sorted(need, key=lambda r: (r not in cnt, -need[r]))
        for final in (False, True):
            for r in order:
                if clk[q].get(r, 0) >= need[r]:
                    continue
                if not final and any(o != r and clk[q].get(o, 0) < need[o] and snap[(o, need[o])].get(r, 0) >= need[r] for o in order):
                    continue
                eng[q].wait_ge(semof(r), need[r])
                learn(q, r, need[r])

    def note(ev, n, reads, writes):
        for reg in writes:
            acc[reg[0]] = [x for x in acc.get(reg[0], []) if not (x[2][1] >= reg[1] and x[2][2] <= reg[2] and (reg[3] == 1 or (x[2][3] == reg[3] and x[2][1] == reg[1])))] + [(ev, n, reg, True)]
        for reg in reads:
            acc[reg[0]] = [x for x in acc.get(reg[0], []) if not (x[0] == ev and not x[3] and x[2] == reg)] + [(ev, n, reg, False)]

    def op(q, fn, outs, ins):
        reads = [r for i in ins for r in i[1]]
        writes = [r for o in outs for r in o[1]]
        sync(q, reads, writes)
        call = fn()
        cnt[q] += 1
        n = cnt[q]
        call.then_inc(semof(q), 1)
        snap[(q, n)] = dict(clk[q])
        snap[(q, n)][q] = n - 1
        note(q, n, reads, writes)

    def sc(x):
        return x[0] if isinstance(x, tuple) else x

    def tl(*xs):
        return [x for x in xs if isinstance(x, tuple)]

    def tt(o, a, b, f): op("V", lambda: eng["V"].tensor_tensor(o[0], a[0], b[0], f), [o], [a, b])
    def ts(o, a, s1, s2, f0, f1=None):
        if f1 is None:
            op("V", lambda: eng["V"].tensor_scalar(o[0], a[0], sc(s1), None, f0), [o], [a] + tl(s1))
        else:
            op("V", lambda: eng["V"].tensor_scalar(o[0], a[0], sc(s1), sc(s2), f0, f1), [o], [a] + tl(s1, s2))
    def cp(o, a): op("V", lambda: eng["V"].tensor_copy(o[0], a[0]), [o], [a])
    def scat(tab, off, a): op("V", lambda: eng["V"].tensor_copy(tab[0].indirect(off[0]), a[0]), [tab], [a, off])
    def scan(o, a, b, i, f0, f1): op("V", lambda: eng["V"].tensor_tensor_scan(o[0], a[0], b[0], i, f0, f1), [o], [a, b])
    def red(o, a): op("V", lambda: eng["V"].tensor_reduce(o[0], a[0], AX.X, A.add), [o], [a])
    def fill(o, c): op("V", lambda: eng["V"].memset(o[0], c), [o], [])
    def act(o, a, f=F.Copy, scale=1.0, bias=0.0):
        op("S", lambda: eng["S"].activation(o[0], a[0], f, bias=sc(bias), scale=sc(scale)), [o], [a] + tl(bias, scale))
    def mm(o, l, r, st=True, sp=True): op("P", lambda: eng["P"].matmul(o[0], l[0], r[0], st, sp), [o], [l, r])
    def iota(o, pat, base, cm, whole=False):
        if whole:
            op("G", lambda: g.iota(o[0], pat, base, cm), [o], [])
        else:
            op("G", lambda: g.iota(o[0], pat, base, cm, allow_small_or_imprecise_dtypes=True), [o], [])
    def asel(o, a, pat, cop, fv, base, cm): op("G", lambda: g.affine_select(o[0], a[0], pat, cop, fv, base, cm), [o], [a])

    def dma(q, sem, out, in_, outs, ins):
        reads, writes = [r for i in ins for r in i[1]], [r for o in outs for r in o[1]]
        sync(q, reads, writes)
        eng[q].dma_start(out, in_).then_inc(T.sem[sem], 16)
        snap[(sem, 16)] = dict(clk[q])
        note(sem, 16, reads, writes)

    def arrive(sem, n, b):
        snap[(sem, n)] = {}
        note(sem, n, [], b[1])

    def send(core, dst, topo, o, i, rsem):
        sync("G", i[1], [])
        rid, pid = topo.addr(dst, core)
        g.remote_dma(o[0], i[0], T.sem[rsem], T.sem.sent, pid, rid, topo.mask(core, dst))
        return len(topo.engines(core, dst))

    return dict(B=B, I=I, tt=tt, ts=ts, cp=cp, scat=scat, scan=scan, red=red, fill=fill, act=act, mm=mm, iota=iota, asel=asel, dma=dma,
                arrive=arrive, send=send, cnt=cnt)


def weave(*lists):
    lists = [list(x) for x in lists]
    while any(lists):
        for x in lists:
            if x:
                x.pop(0)()


def rank_program(g, core, T, topo):
    rank = T.rank_of(core)
    if rank is None:
        return
    K = make(g, T)
    B, I, tt, ts, cp, scat, scan, red, fill, act, mm, iota, asel, dma = (K[k] for k in (
        "B", "I", "tt", "ts", "cp", "scat", "scan", "red", "fill", "act", "mm", "iota", "asel", "dma"))
    nxt = T.cores[(rank + 3) % len(T.cores)]
    prv_eng = len(topo.engines(T.cores[(rank + 1) % len(T.cores)], core))

    def dedupe(c, bank, a, flist, fpos):
        s = str(c)
        own = B("FL", 96 * c + 15, 96 * c + 96, 16)
        return [lambda: tt(B("RMk" + s), B(bank, a, a + 96), B("NEG", 0, 96), A.add),
                lambda: scan(B("FL", 96 * c, 96 * c + 96), B("HOLD", 0, 96), B("RMk" + s), 0.0, A.add, A.max),
                lambda: tt(B("eq" + s, 0, 95), B(bank, a + 1, a + 96), B("FL", 96 * c, 96 * c + 95), A.is_equal),
                lambda: cp(flist, own),
                lambda: scan(B("dup" + s, 0, 95), B("SEG", 0, 95), B("eq" + s, 0, 95), 0.0, A.mult, A.max),
                lambda: ts(B("pT" + s), B("dup" + s, 14, 95, 16), B("TC"), None, A.mult),
                lambda: tt(B("pQ" + s), B("pT" + s), own, A.max),
                lambda: cp(fpos, B("pQ" + s))]

    def marks(tab, val, pos, p0, t, c):
        return [lambda b=b: scat(B(tab), B(pos, p0 + 2 * b, p0 + 2 * b + 1), B(val, 192 * t + 16 * b, 192 * t + 16 * b + 16))
                for b in range(6 * c + 5, 6 * c - 1, -1)]

    dma("Y", "ld0", T.v0s[:], T.v0[:], [B("v0s")], [])
    QW = 512
    for j in range(4):
        dma("Y", "ld%d" % (3 + j), T.enS[:, j * QW:(j + 1) * QW], T.en[:, j * QW:(j + 1) * QW], [B("enS", j * QW, (j + 1) * QW)], [])
    dma("S", "ld1", T.z0s[:], T.z0[:], [B("z0s")], [])
    dma("S", "ld2", T.wts[:], T.wt[:], [B("wts")], [])
    dma("S", "ld7", T.XS[:], T.xs[:], [B("XS")], [])

    fill(B("ones"), 1.0); fill(B("onef"), 1.0); fill(B("GFt"), 32.0); fill(B("GTt"), 1024.0); fill(B("o32"), 1.0 / 32)
    iota(B("qI"), [[0, 1]], 0, 1, True)
    iota(B("CI"), [[0, 12], [1, 16]], 0, 0)
    asel(B("BDt"), B("ones", 0, 128), [[-16, 8], [0, 16]], A.is_ge, 0.0, 0, 1)
    asel(B("BD"), B("BDt"), [[16, 8], [0, 16]], A.is_ge, 0.0, 15, -1)
    asel(B("BAND"), B("ones", 0, 160), [[1, 160]], A.is_equal, 0.0, -16, -1)
    asel(B("GBt"), B("onef", 0, 8), [[-16, 8]], A.is_ge, 0.0, 0, 1)
    asel(B("GB"), B("GBt"), [[16, 8]], A.is_ge, 0.0, 15, -1)
    asel(B("ID"), B("ones", 0, 128), [[-1, 128]], A.is_equal, 0.0, 0, 1)
    iota(B("VAL", 0, 192), [[32, 12], [-2, 16]], 30, 0)
    iota(B("VV", 0, 192), [[32, 12], [-2, 16]], 29, 0)
    asel(B("EXPT"), B("ones", 0, 136), [[-16, 8], [0, 17]], A.is_equal, 0.0, 0, 1)
    iota(B("FV"), [[0, 2064]], 9999, 0)
    ts(B("qJ"), B("qI"), 15, None, A.bitwise_and)
    cp(B("qi"), B("qJ"))
    ts(B("RM16"), B("CI", 0, 16), B("qi"), None, A.is_equal)
    ts(B("WC"), B("RM16"), -2097152.0 + 8192.0, -8192.0, A.mult, A.add)
    act(B("GBs"), B("GB"), scale=2.0 ** -10)
    for i in range(16):
        act(B("selB", 8 * i, 8 * i + 8), B("GBs"), scale=B("RM16", i, i + 1))
        act(B("WN", 8 * i, 8 * i + 8), B("GB"), scale=B("WC", i, i + 1))
    act(B("INK"), B("ID"), scale=-2048.0)
    ts(B("EQD"), B("CI"), B("qi"), None, A.is_equal)
    ts(B("NEG"), B("EQD"), 4096.0, -4096.0, A.mult, A.add)
    fill(B("HOLD"), 0.0); fill(B("SEG"), 1.0); fill(B("OT"), 0); fill(B("MM", 192, 384), 0.0)
    fill(B("HOLD", 0, 192, 16), -8192.0); fill(B("SEG", 0, 192, 16), 0.0)
    cp(B("v0f"), B("v0s"))
    for i in range(16):
        act(B("LM", i, 192, 16), B("v0f"), scale=B("RM16", 15 - i, 16 - i))
    mm(B("pb7", 0, 192), B("BD"), B("LM"))
    act(B("MM", 0, 192), B("pb7", 0, 192))
    ts(B("TC"), B("qi"), 2048.0, None, A.add)
    for i in range(16):
        ts(B("ZI", 160 * i, 160 * i + 160), B("BAND"), B("RM16", i, i + 1), None, A.mult)
    fill(B("NT", 2048, 2432), 0.0); fill(B("ST", 2048, 2432), 0.0)
    for j in range(4):
        a, b = j * QW, (j + 1) * QW
        ts(B("tmpB", a, b), B("enS", a, b), 1.0 / 2048, 159.5 + 1.0 / 8192, A.mult, A.add)
        act(B("ST", a, b), B("tmpB", a, b), bias=-160.0)
        mm(B("pb%d" % j), B("INK"), B("ST", a, b))
    for i in range(16):
        act(B("Zz", i, 192, 16), B("z0s", 15 - i, 192, 16))
    weave(*[dedupe(c, "pb7", 96 * c, B("RT", 6 * c, 6 * c + 6), B("RT", 12 + 12 * c, 24 + 12 * c, 2)) for c in CH])
    ts(B("qs1"), B("qi"), 1.0, None, A.add)
    cp(B("wtf"), B("wts"))
    ts(B("q15"), B("qi"), 15.0, None, A.is_equal)
    ts(B("qK"), B("qJ"), 1, None, A.bitwise_and)
    ts(B("qe"), B("qK"), -1.0, 1.0, A.mult, A.add)
    tt(B("w1"), B("qe"), B("q15"), A.add)
    ts(B("qo"), B("w1"), -1.0, 1.0, A.mult, A.add)
    act(B("W16"), B("GB"), scale=1024.0)
    act(B("WD"), B("GB"), scale=B("wtf"))
    act(B("IDb"), B("ID")); act(B("I22"), B("ID"), scale=4194304.0)
    for j in range(4):
        a, b = j * QW, (j + 1) * QW
        tt(B("NT", a, b), B("enS", a, b), B("pb%d" % j), A.add)

    def consts_late(part):
        if part:
            iota(B("FF"), [[0, 2064]], 9999, 0)
            for t in range(1, HOPS):
                iota(B("VAL", 192 * t, 192 * t + 192), [[32, 12], [-2, 16]], 30 - 512 * t, 0)
                iota(B("VV", 192 * t, 192 * t + 192), [[32, 12], [-2, 16]], 29 - 512 * t, 0)
            return
        asel(B("SELT"), B("o32"), [[-16, 8], [-1, 17]], A.is_equal, 0.0, 1, 1)
        iota(B("KTHR"), [[0, 8], [-1, 17]], 17, 0)
        iota(B("BK"), [[0, 8], [64, 17]], -64, 0)
        asel(B("GF", 0, 128, 1, 0, 16), B("GFt", 0, 128, 1, 0, 16), [[-1, 8], [0, 16]], A.is_equal, 0.0, 0, 1)
        asel(B("GT", 0, 128, 1, 0, 16), B("GTt", 0, 128, 1, 0, 16), [[-1, 8], [0, 16]], A.is_equal, 0.0, -8, 1)
        iota(B("TRb"), [[1, 24]], 2048, 0)

    def consts_v1():
        return [lambda: fill(B("SELT", 0, 136, 17), 0.0), lambda: fill(B("BK", 0, 136, 17), -524288.0),
                lambda: fill(B("RST"), -1.0e7), lambda: fill(B("RST", 0, 136, 17), 1.0e7)]

    def consts_v2():
        return [lambda: ts(B("q24"), B("qi"), 24.0, None, A.mult), lambda: ts(B("TR"), B("TRb"), B("q24"), None, A.add),
                lambda: ts(B("OFFD"), B("EQD"), 1.0e6, -1.0e6, A.mult, A.add),
                lambda: tt(B("OWN", 0, 192), B("VAL", 0, 192), B("OFFD"), A.add)]

    def consts_s():
        act(B("NID"), B("ID"), scale=-1.0); act(B("P64"), B("ID"), scale=64.0); act(B("N64"), B("ID"), scale=-64.0)
        act(B("DE"), B("ID"), scale=B("qe")); act(B("DO"), B("ID"), scale=B("qo")); act(B("D15"), B("ID"), scale=B("q15"))
        act(B("DEb"), B("ID"), scale=B("qe")); act(B("DOb"), B("ID"), scale=B("qo"))
        for t in range(HOPS):
            act(B("BT", t, t + 1), B("q15"), scale=9.0 + t)
        act(B("I2K"), B("ID"), scale=2048.0)
        act(B("GBy"), B("GB"), scale=2048.0)
        act(B("YWn"), B("GB"), scale=B("qs1")); act(B("YWs"), B("GBy"), scale=B("qs1"))

    sent = 0
    held = []
    for t in range(HOPS):
        last = t == HOPS - 1
        zc, mc, rc = 192 * t, 384 * t, 40 * t
        if t > 0:
            K["arrive"]("aL%d" % t, prv_eng, B("RT", rc, rc + 36))
            K["arrive"]("aM%d" % t, prv_eng, B("MM", mc, mc + 384))
            for c in CH:
                K["arrive"]("aZ%d%d" % (c, t), prv_eng, B("Zz", zc + 96 * c, zc + 96 * c + 96))
        vl, fl = B("RT", rc, rc + 12), B("OT", rc, rc + 12)

        def W(n, a=0, b=16, st=1):
            return B(n, a, b, st, 0, 96)

        def bc(name, c, k):
            return B(name, 1536 * c + k, 1536 * c + 1536, 16)

        def gat(c, what):
            act(B(what, 1536 * c, 1536 * c + 1536), I(B("NT" if what == "X" else "ST"), B("RL", 96 * c, 96 * c + 96)))

        def selx(c):
            for k in range(16):
                i = (k + t) % 16
                off = 160 * i + 16 - (k - i)
                mm(B("pb4", 96 * c, 96 * c + 96), B("ZI", off, off + 128), bc("X", c, k), k == 0, k == 15)

        def lists(c):
            cp(B("AL", 96 * c, 96 * c + 96), B("pb4", 96 * c, 96 * c + 96))
            cp(B("CN", 96 * c, 96 * c + 96), B("AL", 96 * c, 96 * c + 96))

        def rec(c):
            tt(B("D", 1536 * c, 1536 * c + 1536), I(B("XS"), B("AL", 96 * c, 96 * c + 96)), B("ZE", 1536 * c, 1536 * c + 1536), A.subtract)

        def size(c):
            act(B("AB", 1536 * c, 1536 * c + 1536), B("D", 1536 * c, 1536 * c + 1536), F.Abs)

        def newer(c):
            return [lambda k=k: tt(bc("M", c, k), bc("S", c, k), B("pb5", 96 * c, 96 * c + 96), A.is_gt) for k in range(16)]

        def pay(c):
            mm(W("pb%d" % (2 + c), 0, 136), B("CN", 96 * c, 96 * c + 96), B("SELT"), True, False)
            for k in range(16):
                i = (k + t) % 16
                mm(W("pb%d" % (2 + c), 1 + k, 136, 17), bc("S", c, k), B("selB", 8 * i, 8 * i + 8), False, False)

        def failcol(c):
            mm(W("pb%d" % (2 + c), 0, 136, 17), W("ID", 0, 96), W("ff", 8 * c, 8 * c + 8), False, True)

        def key0(c):
            mm(W("pb%d" % c, 0, 136), W("IDb", 0, 96), W("BK", 0, 136), True, False)
            mm(W("pb%d" % c, 0, 136), W("I22", 0, 96), W("TBc", 136 * c, 136 * c + 136), False, False)

        def keyA(c):
            for k in range(16):
                mm(W("pb%d" % c, 1 + k, 136, 17), bc("AB", c, k), B("W16"), False, False)

        def keyM(c):
            for k in range(16):
                i = (k + t) % 16
                mm(W("pb%d" % c, 1 + k, 136, 17), bc("M", c, k), B("WN", 8 * i, 8 * i + 8), False, k == 15)

        def zexp(c, q, k0, k1):
            for k in range(k0, k1):
                z = B("Zz", zc + 96 * c, zc + 96 * c + 96)
                if q == "G":
                    asel(bc("ZE", c, k), z, [[0, 96]], A.is_equal, 0.0, 0, 0)
                elif q == "S":
                    act(bc("ZE", c, k), z)
                else:
                    cp(bc("ZE", c, k), z)

        def tail(c):
            s = str(c)
            kk, pp = W("pb%d" % c, 0, 136), W("pb%d" % (2 + c), 0, 136)
            mn, dd, ee, oo = (W(n + s, 0, 136) for n in ("Mn", "dd", "ee", "oo"))
            o16 = W("oo" + s, 16, 136, 17)
            return [lambda: scan(mn, W("RST", 0, 136), kk, 0.0, A.max, A.min), lambda: tt(dd, kk, mn, A.subtract),
                    lambda: tt(ee, pp, dd, A.subtract), lambda: scan(oo, dd, ee, 0.0, A.min, A.max),
                    lambda: ts(W("WT" + s, 0, 8), o16, 393216.0, 393216.0, A.add, A.subtract),
                    lambda: tt(W("WT" + s, 8, 16), o16, W("WT" + s, 0, 8), A.subtract)]

        def turn(c):
            q = B("pb6", 320 + 96 * c, 416 + 96 * c, 1, 0, 16)
            tp = B("TPs", 96 * c, 96 * c + 96, 1, 0, 16)
            mm(q, W("WT%d" % c, 0, 16), W("ID", 0, 96))
            act(tp, q)
            mm(B(RB[c], 0, 96), B("GF", 0, 128, 1, 0, 16), tp)
            mm(B(RB[c], 96, 192), B("GT", 0, 128, 1, 0, 16), tp)

        def share(c):
            for k in (0, 1):
                act(B("MO", mc + 192 * k + 96 * c, mc + 192 * k + 96 * c + 96), B(RB[c], 96 * k, 96 * k + 96))

        def zproc(c):
            a, b = 96 * c, 96 * c + 96
            zt = B("Zz", zc + a, zc + b)
            act(B("FM", a, b), B(RB[c], 96, 192), F.Relu, scale=-1.0, bias=1.0)
            act(B("XF", a, b), I(B("XS"), B("OT", rc + 6 * c, rc + 6 * c + 6)))
            mm(B("pb1", a, b), B("ID"), zt, True, False)
            mm(B("pb1", a, b), B("NID"), B("XF", a, b), False, True)
            mm(B("pb3", a, b), B("ID"), zt, True, False)
            mm(B("pb3", a, b), B("N64"), B("FM", a, b), False, True)
            act(B("AZ", a, b), B("pb1", a, b), F.Abs)
            act(B("R1", a, b), B("pb3", a, b), F.Relu)
            mm(B("pb3", 192 + a, 192 + b), B("ID"), B("AZ", a, b), True, False)
            mm(B("pb3", 192 + a, 192 + b), B("P64"), B("FM", a, b), False, True)
            act(B("R2", a, b), B("pb3", 192 + a, 192 + b), F.Relu, bias=-64.0)
            mm(B("pb1", 192 + a, 192 + b), B("ID"), B("R1", a, b), True, False)
            mm(B("pb1", 192 + a, 192 + b), B("ID"), B("R2", a, b), False, True)
            if not last:
                act(B("ZO", zc + a, zc + b), B("pb1", 192 + a, 192 + b))

        def out(o, src, n, a, b, sem):
            if last:
                return 0
            return K["send"](core, nxt, topo, B(o, n * (t + 1) + a, n * (t + 1) + b), B(src, n * t + a, n * t + b), sem + str(t + 1))

        for c in CH:
            cp(B("RL", 96 * c, 96 * c + 96), I(B("NT"), B("RT", rc + 6 * c, rc + 6 * c + 6)))
        act(B("X", 1536, HX), I(B("NT"), B("RL", 96, HR)))
        cp(B("X", HX, 3072), I(B("NT"), B("RL", HR, 192)))
        for f_ in held:
            f_()
        zexp(1, "S", G1 + V1, 16)
        gat(0, "X"); gat(1, "S")
        zexp(0, "S", G0, 16)
        mm(B("pb5", 0, 192), B("ID"), B("MM", mc + 192, mc + 384))
        for c in (0, 1):
            mm(W("pb6", 136 * c, 136 * c + 136), B("MM", mc + 192 + 96 * c, mc + 288 + 96 * c), B("EXPT"))
        selx(1)
        zexp(1, "G", 0, G1)
        if t == 0:
            consts_late(0)
        zexp(0, "G", 0, G0)
        if t == 0:
            consts_late(1)
        e1, e2 = [], []
        for c in (0, 1):
            e1.append(lambda c=c: tt(W("TBc", 136 * c, 136 * c + 136), W("pb6", 136 * c, 136 * c + 136), W("KTHR", 0, 136), A.is_ge))
        e1.append(lambda: cp(B("vlf"), vl))
        if t > 0:
            e1.append(lambda: red(W("Af", 0, 1), W("pb3", 480, 496)))
            e1.append(lambda: cp(W("Ai", 0, 1), W("Af", 0, 1)))
            e1.append(lambda: ts(W("Aj", 0, 1), W("Ai", 0, 1), 255, None, A.bitwise_and))
            e1.append(lambda: cp(W("Ac", 0, 1), W("Aj", 0, 1)))
        else:
            e1.append(lambda: fill(B("Ac"), 0.0))
        e2.append(lambda: cp(W("ui"), W("pb6", 288, 304)))
        e2.append(lambda: ts(W("ua"), W("ui"), 2047, None, A.bitwise_and))
        e2.append(lambda: tt(W("ub"), W("ua"), W("ua"), A.mult))
        e2.append(lambda: ts(W("ud"), W("ua"), 37.0, W("Ac", 0, 1), A.mult, A.add))
        e2.append(lambda: ts(W("uc"), W("ub"), 5, None, A.arith_shift_right))
        e2.append(lambda: tt(W("ue"), W("uc"), W("ud"), A.add))
        e2.append(lambda: ts(W("uf"), W("ue"), 2047, None, A.bitwise_and))
        e2.append(lambda: ts(W("ff"), W("uf"), 1.0 / 32, None, A.mult))
        weave([lambda k=k: zexp(1, "V", k, k + 1) for k in range(G1, G1 + V1)], consts_v1() if t == 0 else [])
        lists(1); rec(1)
        size(1)
        gat(0, "S")
        pay(1)
        n1 = newer(1)
        weave(n1[:8], e1)
        for c in (0, 1):
            mm(W("pb6", 288 + 8 * c, 296 + 8 * c), B("Zz", zc + 96 * c, zc + 96 * c + 96), B("WD"))
        weave(n1[8:], e2)
        selx(0)
        key0(1); keyA(1); keyM(1)
        failcol(1)
        lists(0); rec(0)
        pay(0); key0(0); failcol(0)
        weave(consts_v2() if t == 0 else [])
        size(0)
        n0 = newer(0)
        weave(n0[:6], tail(1))
        turn(1)
        weave(n0[6:], marks("FV", "VV", "RT", rc + 12, t, 1) + marks("FV", "VV", "RT", rc + 12, t, 0))
        keyA(0); keyM(0)
        act(B("Rv"), I(B("NT"), vl))
        act(B("Sv"), I(B("ST"), vl))
        if t > 0:
            act(B("OWN", zc, zc + 192), B("OWN", 0, 192), bias=-512.0 * t)
        else:
            consts_s()
        share(1)
        act(B("G0"), I(B("FV"), vl), bias=1.0)
        weave(tail(0), dedupe(1, RB[1], 0, B("OT", rc + 6, rc + 12), B("OT", rc + 24, rc + 36, 2)))
        turn(0)
        share(0)
        zproc(1)
        sent += out("Zz", "ZO", 192, 96, 192, "aZ1")
        m1 = marks("FF", "VAL", "OT", rc + 12, t, 1)
        weave(m1[:3], [lambda c=c: ts(W("FC", 8 * c, 8 * c + 8), W("WT%d" % c, 8, 16), 0.0, None, A.is_equal) for c in (0, 1)])
        weave(dedupe(0, RB[0], 0, B("OT", rc, rc + 6), B("OT", rc + 12, rc + 24, 2)), m1[3:])
        sent += out("MM", "MO", 384, 0, 384, "aM")
        sent += out("RT", "OT", 40, 0, 36, "aL")
        act(B("Rf"), I(B("NT"), fl))
        act(B("Sf"), I(B("ST"), fl))
        weave(marks("FF", "VAL", "OT", rc + 12, t, 0), [lambda: tt(B("pre"), I(B("FV"), fl), B("G0"), A.min)])
        vr, fr = B("MM", mc, mc + 192), B("MO", mc, mc + 192)
        for h, (own, oth, new) in enumerate((("Rv", "Rf", fr), ("Rf", "Rv", vr))):
            o = B("pb0", 192 * h, 192 * h + 192)
            mm(o, B("DO"), B(own), True, False)
            mm(o, B("D15"), new, False, False)
            mm(o, B("DE"), B(oth), False, True)
        act(B("NNs"), B("pb0", 0, 384))
        for h, (own, oth) in enumerate((("Sv", "Sf"), ("Sf", "Sv"))):
            o = B("pb2", 192 * h, 192 * h + 192)
            mm(o, B("DOb"), B(own), True, False)
            mm(o, B("DEb"), B(oth), False, True)
        act(B("NSs"), B("pb2", 0, 384), F.Identity, bias=B("BT", t, t + 1))
        tt(B("ma"), I(B("FF"), vl), B("pre"), A.min)
        tt(B("mb"), I(B("FF"), fl), B("ma"), A.min)
        tt(B("nd"), B("mb"), B("OWN", zc, zc + 192), A.is_lt)
        scan(B("ns"), B("SEG"), B("nd"), 0.0, A.mult, A.max)
        nl = B("ns", 15, 192, 16)
        tt(B("nT", 0, 12), nl, B("TR", 0, 12), A.mult)
        tt(B("nT", 12, 24), nl, B("TR", 12, 24), A.mult)
        tt(B("nP", 0, 12), B("nT", 0, 12), B("vlf"), A.max)
        tt(B("nP", 12, 24), B("nT", 12, 24), B("FL", 15, 192, 16), A.max)
        cp(B("POS"), B("nP"))
        held = [lambda: scat(B("ST"), B("POS"), B("NSs"))]
        if last:
            held[0]()
        scat(B("NT"), B("POS"), B("NNs"))
        zproc(0)
        if not last:
            sent += out("Zz", "ZO", 192, 0, 96, "aZ0")
            mm(W("pb3", 480, 496), W("ones", 0, 96), W("FC"))

    mc = 384 * (HOPS - 1)
    mm(B("pb7", 256, 448), B("ID"), B("MO", mc, mc + 192), True, False)
    mm(B("pb7", 256, 448), B("I2K"), B("MO", mc + 192, mc + 384), False, True)
    YB = ("pb2", "pb5", "pb4", "pb0")
    for j in range(4):
        mm(B(YB[j], 0, 512, 1, 0, 8), B("YWs"), B("ST", 512 * j, 512 * j + 512), True, False)
    for i in range(16):
        act(B("YP", 15 - i, 192, 16), B("pb7", 256 + i, 448, 16))
    dma("Y", "st1", T.yp[:], T.YP[0:128:16, :], [], [B("YP")])
    for j in range(4):
        a, b = 512 * j, 512 * j + 512
        if j % 2:
            act(B("NTh", a, b), B("NT", a, b))
        else:
            cp(B("NTh", a, b), B("NT", a, b))
    for j in range(4):
        mm(B(YB[j], 0, 512, 1, 0, 8), B("YWn"), B("NTh", 512 * j, 512 * j + 512), False, True)
    for j in range(4):
        a, b = 512 * j, 512 * j + 512
        o = B(YB[j], 0, 512, 1, 0, 8)
        if j % 2:
            act(B("YS", a, b, 1, 0, 8), o)
        else:
            cp(B("YS", a, b, 1, 0, 8), o)
    dma("Y", "st2", T.ys[:], T.YS[0:8, :], [], [B("YS")])
    for i in range(16):
        act(B("YZ", 15 - i, 192, 16), B("pb1", 192 + i, 384, 16))
    dma("Y", "st0", T.yz[:], T.YZ[:], [], [B("YZ")])

    for q in ("V", "S", "P", "G"):
        g.wait_ge(T.sem["c" + q], K["cnt"][q])
    for j in range(8):
        g.wait_ge(T.sem["ld%d" % j], 16)
    for j in range(3):
        g.wait_ge(T.sem["st%d" % j], 16)
    g.wait_ge(T.sem.sent, sent)
